import numpy as np
import ml_dtypes


def mxq(x, axis, fmt="e4m3"):
    dtype, down = {"e4m3": (ml_dtypes.float8_e4m3fn, 7), "e5m2": (ml_dtypes.float8_e5m2, 14)}[fmt]
    v = np.moveaxis(np.asarray(x, np.float32).astype(ml_dtypes.bfloat16).astype(np.float64), axis, -1)
    blocks = v.reshape(v.shape[:-1] + (-1, 32))
    amax = np.abs(blocks).max(-1, keepdims=True)
    byte = np.maximum(np.where(amax > 0, np.frexp(amax)[1] - 1 + 127, 0) - down, 1)
    scale = np.exp2(byte - 127.0)
    codes = (blocks / scale).astype(np.float32).astype(dtype).astype(np.float64)
    return np.moveaxis((codes * scale).reshape(v.shape), -1, axis)


WIDE = False


def mx_kscale(k):
    if not WIDE:
        return np.ones(k)
    levels = np.array([30, -30])
    if k % 512:
        return np.exp2(np.random.permutation(np.resize(levels, k // 32))).repeat(32)
    a = np.empty((k // 512, 16))
    for p in range(k // 512):
        a[p, :8] = np.random.permutation(np.resize(levels, 8))
        for g in range(8):
            far = levels[np.abs(levels - a[p, g]) >= 10]
            a[p, g + 8] = far[np.random.randint(len(far))]
    return np.exp2(a.ravel()).repeat(32)


def f64(x):
    return np.asarray(x).astype(np.float64)


def striped(idx):
    return np.tile(np.asarray(idx).reshape(-1, 16).T, (8, 1)).astype(np.uint16)


def unstriped(offs):
    return offs[:16].T.reshape(-1).astype(np.int64)


E2M1 = np.array([0.0, 0.5, 1.0, 1.5, 2.0, 3.0, 4.0, 6.0, -0.0, -0.5, -1.0, -1.5, -2.0, -3.0, -4.0, -6.0])


def pack_weight(w, fmt):
    k, n = w.shape
    w = f64(np.asarray(w, np.float32).astype(ml_dtypes.bfloat16)).reshape(k // 32, 32, n)
    amax = np.abs(w).max(1)
    if fmt in ("e4m3", "e5m2"):
        byte = np.frexp(amax)[1] - 1 + 127 - (7 if fmt == "e4m3" else 14)
    else:
        mant, ex = np.frexp(amax / 6.0)
        byte = np.where(mant > 0.5, ex, ex - 1) + 127
    byte = np.clip(np.where(amax > 0, byte, 1), 1, 254)
    scaled = (w * np.exp2(127.0 - byte)[:, None, :]).reshape(k, n).astype(np.float32)
    by_word = np.ascontiguousarray(scaled.reshape(k // 512, 128, 4, n).transpose(0, 1, 3, 2))
    if fmt in ("e4m3", "e5m2"):
        words = by_word.astype(ml_dtypes.float8_e4m3fn if fmt == "e4m3" else ml_dtypes.float8_e5m2).view(np.uint8)
    else:
        c = by_word.astype(ml_dtypes.float4_e2m1fn).view(np.uint8) & 0xF
        words = (c[..., 0::2] | (c[..., 1::2] << 4)).reshape(k // 512, 128, 2 * n)
    return np.ascontiguousarray(words), np.ascontiguousarray(byte.astype(np.uint8).reshape(k // 512, 16, n))


def unpack_weight(words, scales, fmt):
    g, _, n = scales.shape
    words = np.ascontiguousarray(words).reshape(g, 128, n, -1)
    if fmt in ("e4m3", "e5m2"):
        vals = words.view(ml_dtypes.float8_e4m3fn if fmt == "e4m3" else ml_dtypes.float8_e5m2).astype(np.float64)
    else:
        nib = np.empty((g, 128, n, 4), np.uint8)
        nib[..., 0::2] = words & 0xF
        nib[..., 1::2] = words >> 4
        vals = E2M1[nib]
    vals = vals * np.repeat(np.exp2(scales.astype(np.float64) - 127.0), 8, axis=1)[..., None]
    return vals.transpose(0, 1, 3, 2).reshape(g * 512, n)


def bf(x):
    return np.asarray(x, np.float32).astype(ml_dtypes.bfloat16)


def planes(Y):
    r, m = Y.shape
    b = f64(bf(Y)).reshape(r // 32, 32, m)
    amax = np.abs(b).max(1)
    byte = np.clip(np.where(amax > 0, np.frexp(amax)[1] - 1 + 127 - 7, 1), 1, 254)
    codes = (b * np.exp2(127.0 - byte)[:, None, :]).reshape(r, m).astype(np.float32).astype(ml_dtypes.float8_e4m3fn).view(np.uint8)
    words = codes.reshape(r // 512, 128, 4, m).transpose(0, 1, 3, 2)
    return np.ascontiguousarray(words), np.ascontiguousarray(byte.astype(np.uint8).reshape(r // 512, 16, m))


K, T, J, R, N = 512, 1024, 256, 512, 512


def setup_inputs():
    n = np.random.standard_normal
    idx = np.random.permutation(T)[:J]
    idx2 = np.random.permutation(T)[:J]
    fk = mx_kscale(K)
    fr = mx_kscale(R)
    wp = pack_weight(n((K, R)) * 1 / np.sqrt(K) * fk[:, None] * fr, "e5m2")
    return {
        "xf": (n((K, T))).astype(np.float32),
        "fk": (np.random.uniform(0.5, 2.0, (K, 1)) / fk[:, None]).astype(np.float32),
        "w_words": wp[0],
        "w_scales": wp[1],
        "wb": (n((R, N)) * 1 / np.sqrt(R) / fr[:, None]).astype(np.float32),
        "rs": (n((N, J))).astype(np.float32),
        "offs": striped(idx),
        "offs2": striped(idx2),
    }


def reference(xf, fk, w_words, w_scales, wb, rs, offs, offs2):
    idx = unstriped(offs)
    idx2 = unstriped(offs2)
    wu = unpack_weight(w_words, w_scales, "e5m2")
    u = np.maximum(f64(xf)[:, idx], f64(xf)[:, idx2]) * f64(fk)
    uq = mxq(u, 0, "e4m3")
    a = wu.T @ uq
    ha = np.maximum(a, 0.0)
    h1 = np.pad(ha, ((0, 0), (2, 0)))[:, :J]
    hid = ha - 0.5 * h1
    wbq = mxq(f64(wb), 0, "e4m3")
    hidq = mxq(hid, 0, "e5m2")
    p = wbq.T @ hidq
    p1 = np.pad(p, ((0, 0), (1, 0)))[:, :J]
    y = p - 0.7 * p1 + 0.5 * f64(rs)
    words, scales = planes(y)
    return y, words, scales

@@ -1,0 +1,196 @@
+from contextlib import ExitStack
+
+import concourse.mybir as mybir
+
+K, T, J, R, N = 512, 1024, 256, 512, 512
+FLOPS = 2 * K * R * J + 2 * R * N * J
+
+F32 = mybir.dt.float32
+BF16 = mybir.dt.bfloat16
+I32 = mybir.dt.int32
+U16 = mybir.dt.uint16
+U8 = mybir.dt.uint8
+E4M3 = mybir.dt.float8_e4m3fn_x4
+E5M2 = mybir.dt.float8_e5m2_x4
+ALU = mybir.AluOpType
+ACT = mybir.ActivationFunctionType
+
+P = 128
+PACK = 4
+CHUNK = 128
+CHUNKS = J // CHUNK
+LIST_COLS = CHUNK // 16
+HID_LAG = 2
+
+
+def tile_list_largerpicks_lagged_lagged_pl_kernel(tc, xf, fk, w_words, w_scales, wb, rs, offs, offs2, out_0, out_1, out_2):
+    nc = tc.nc
+    with ExitStack() as ctx:
+        pool = ctx.enter_context(tc.tile_pool(name="sbuf", bufs=1))
+        psum = ctx.enter_context(tc.psum_pool(name="psum", bufs=1))
+
+        def slots(c):
+            return slice(c * CHUNK, (c + 1) * CHUNK)
+
+        list_a = pool.tile([P, J // 16], U16, name="list_a")
+        list_b = pool.tile([P, J // 16], U16, name="list_b")
+        x = [pool.tile([P, T], F32, name="x%d" % t) for t in range(PACK)]
+        factor = pool.tile([P, PACK], F32, name="factor")
+        w_raw = pool.tile([P, R], I32, name="w_raw")
+        w_scale_raw = pool.tile([P, R], U8, name="w_scale_raw")
+        wb_raw = [pool.tile([P, PACK, N // 2], F32, name="wb_raw%d" % h) for h in range(2)]
+        resid = pool.tile([P, PACK, J], F32, name="resid")
+        half_relu = pool.tile([P, J, PACK], F32, name="half_relu")
+
+        nc.vector.memset(w_scale_raw[:].bitcast(I32), 0)
+        nc.vector.memset(half_relu[:, 0:HID_LAG, :], 0.0)
+
+        x_rows = xf.rearrange("(p t) n -> p t n", t=PACK)
+        wb_rows = wb.rearrange("(p t) n -> p t n", t=PACK)
+        nc.sync.dma_start(x[0][:], x_rows[:, 0, :])
+        nc.sync.dma_start(list_a[:], offs)
+        nc.sync.dma_start(list_b[:], offs2)
+        nc.sync.dma_start(factor[:], fk.rearrange("(p t) o -> p (t o)", t=PACK))
+        nc.sync.dma_start(x[1][:], x_rows[:, 1, :])
+        nc.sync.dma_start(x[2][:], x_rows[:, 2, :])
+        for q in range(4):
+            nc.sync.dma_start(w_scale_raw[:].bitcast(I32)[32 * q : 32 * q + 4, :], w_scales[0, 4 * q : 4 * q + 4, :].bitcast(I32))
+        nc.sync.dma_start(x[3][:], x_rows[:, 3, :])
+        nc.sync.dma_start(w_raw[:], w_words[0].rearrange("p n t -> p (n t)").bitcast(I32))
+        for h in range(2):
+            nc.sync.dma_start(wb_raw[h][:], wb_rows[:, :, h * (N // 2) : (h + 1) * (N // 2)])
+        nc.sync.dma_start(resid[:], rs.rearrange("(p t) j -> p t j", t=PACK))
+
+        pick_a = [pool.tile([P, J], F32, name="pick_a%d" % t) for t in range(PACK)]
+        pick_b = [pool.tile([P, J], F32, name="pick_b%d" % t) for t in range(PACK)]
+        larger = [pool.tile([P, J], F32, name="larger%d" % t) for t in range(PACK)]
+        u_bf = pool.tile([P, J, PACK], BF16, name="u_bf", align_bytes=64)
+        u_codes = pool.tile([P, J], I32, name="u_codes", align_bytes=64)
+        u_scales = pool.tile([P, J], U8, name="u_scales", align_bytes=64)
+        w_codes = pool.tile([P, R], I32, name="w_codes", align_bytes=64)
+        w_scale = pool.tile([P, R], U8, name="w_scale", align_bytes=64)
+
+        def entries(lst, c):
+            return lst[:, c * LIST_COLS : (c + 1) * LIST_COLS]
+
+        def keep_larger(t, cols):
+            nc.vector.tensor_tensor(larger[t][:, cols], pick_a[t][:, cols], pick_b[t][:, cols], ALU.max)
+
+        def scale_and_round(t, cols):
+            nc.vector.tensor_scalar(u_bf[:, cols, t], larger[t][:, cols], factor[:, t : t + 1], None, ALU.mult)
+
+        def quantize(codes, scales, src, cols, fmt):
+            nc.vector.quantize_mx(codes[:, cols].bitcast(fmt), scales[:, cols], src.rearrange("p j t -> p (j t)"))
+
+        every = slice(0, J)
+        for t in range(PACK - 1):
+            nc.scalar.activation(pick_a[t][:], x[t][:].indirect(list_a[:]), ACT.Copy)
+            nc.scalar.activation(pick_b[t][:, slots(1)], x[t][:].indirect(entries(list_b, 1)), ACT.Copy)
+            nc.vector.tensor_copy(pick_b[t][:, slots(0)], x[t][:].indirect(entries(list_b, 0)))
+            if t > 0:
+                scale_and_round(t - 1, every)
+            keep_larger(t, every)
+        nc.vector.tensor_copy(
+            w_scale[:].rearrange("p (t m) -> p t m", t=PACK), w_scale_raw[:].rearrange("p (m t) -> p t m", t=PACK)
+        )
+        last = PACK - 1
+        scale_and_round(last - 1, every)
+        nc.scalar.activation(pick_a[last][:, slots(0)], x[last][:].indirect(entries(list_a, 0)), ACT.Copy)
+        nc.vector.tensor_copy(pick_b[last][:, slots(0)], x[last][:].indirect(entries(list_b, 0)))
+        nc.scalar.activation(pick_a[last][:, slots(1)], x[last][:].indirect(entries(list_a, 1)), ACT.Copy)
+        nc.scalar.activation(pick_b[last][:, slots(1)], x[last][:].indirect(entries(list_b, 1)), ACT.Copy)
+
+        keep_larger(last, slots(0))
+        scale_and_round(last, slots(0))
+        nc.vector.tensor_copy(
+            w_codes[:].rearrange("p (t c i) -> p c t i", t=PACK, i=4), w_raw[:].rearrange("p (c i t) -> p c t i", t=PACK, i=4)
+        )
+        quantize(u_codes, u_scales, u_bf[:, slots(0), :], slots(0), E4M3)
+        keep_larger(last, slots(1))
+        scale_and_round(last, slots(1))
+        quantize(u_codes, u_scales, u_bf[:, slots(1), :], slots(1), E4M3)
+
+        def product(bank, codes, scales, fmt, rhs_codes, rhs_scales, rhs_fmt, c):
+            for t in range(PACK):
+                cols = slice(t * P, (t + 1) * P)
+                nc.tensor.matmul_mx(
+                    bank[:, t, :],
+                    lhsT=codes[:, cols].bitcast(fmt),
+                    lhsT_scale=scales[:, cols],
+                    rhs=rhs_codes[:, slots(c)].bitcast(rhs_fmt),
+                    rhs_scale=rhs_scales[:, slots(c)],
+                    start=True,
+                    stop=True,
+                )
+
+        a_bank = [psum.tile([P, PACK, CHUNK], F32, name="a_bank%d" % c) for c in range(CHUNKS)]
+        p_bank = [psum.tile([P, PACK, CHUNK], F32, name="p_bank%d" % c) for c in range(CHUNKS)]
+        hid_bf = [pool.tile([P, CHUNK, PACK], BF16, name="hid_bf%d" % c, align_bytes=64) for c in range(CHUNKS)]
+        hid_codes = pool.tile([P, J], I32, name="hid_codes", align_bytes=64)
+        hid_scales = pool.tile([P, J], U8, name="hid_scales", align_bytes=64)
+        wb_bf = pool.tile([P, PACK, P, PACK], BF16, name="wb_bf", align_bytes=64)
+        wb_codes = pool.tile([P, N], I32, name="wb_codes", align_bytes=64)
+        wb_scales = pool.tile([P, N], U8, name="wb_scales", align_bytes=64)
+
+        def round_wb(h):
+            nc.scalar.copy(
+                wb_bf[:, :, h * 64 : (h + 1) * 64, :].rearrange("p t m i -> p m t i"),
+                wb_raw[h][:].rearrange("p i (m t) -> p m t i", t=PACK),
+            )
+
+        def relu_half(c):
+            width = min(CHUNK, J - HID_LAG - c * CHUNK)
+            first = c * CHUNK + HID_LAG
+            nc.scalar.activation(
+                half_relu[:, first : first + width, :], a_bank[c][:, :, 0:width].rearrange("p t j -> p j t"), ACT.Relu, scale=0.5
+            )
+
+        def make_hid(c):
+            nc.vector.scalar_tensor_tensor(
+                hid_bf[c][:], a_bank[c][:].rearrange("p t j -> p j t"), 0.0, half_relu[:, slots(c), :], ALU.max, ALU.subtract
+            )
+
+        for c in range(CHUNKS):
+            product(a_bank[c], w_codes, w_scale, E5M2, u_codes, u_scales, E4M3, c)
+        relu_half(0)
+        round_wb(0)
+        relu_half(1)
+        round_wb(1)
+        make_hid(0)
+        make_hid(1)
+        quantize(hid_codes, hid_scales, hid_bf[0][:], slots(0), E5M2)
+        quantize(hid_codes, hid_scales, hid_bf[1][:], slots(1), E5M2)
+        nc.vector.quantize_mx(wb_codes[:].bitcast(E4M3), wb_scales[:], wb_bf[:].rearrange("p t m i -> p (t m i)"))
+        for c in range(CHUNKS):
+            product(p_bank[c], wb_codes, wb_scales, E4M3, hid_codes, hid_scales, E5M2, c)
+
+        y = [pool.tile([P, PACK, CHUNK], F32, name="y%d" % c) for c in range(CHUNKS)]
+        y_bf = [pool.tile([P, CHUNK, PACK], BF16, name="y_bf%d" % c, align_bytes=64) for c in range(CHUNKS)]
+        y_codes = pool.tile([P, J], I32, name="y_codes", align_bytes=64)
+        y_scales = pool.tile([P, J], U8, name="y_scales", align_bytes=64)
+        out_rows = out_0.rearrange("(p t) j -> p t j", t=PACK)
+        out_words = out_1[0].rearrange("p c t -> p (c t)").bitcast(I32)
+
+        def take_lagged(c):
+            width = min(CHUNK, J - 1 - c * CHUNK)
+            cols = slice(c * CHUNK + 1, c * CHUNK + 1 + width)
+            nc.vector.scalar_tensor_tensor(resid[:, :, cols], p_bank[c][:, :, 0:width], -1.4, resid[:, :, cols], ALU.mult, ALU.add)
+
+        def finish(c):
+            nc.vector.scalar_tensor_tensor(y[c][:], resid[:, :, slots(c)], 0.5, p_bank[c][:], ALU.mult, ALU.add)
+            nc.sync.dma_start(out_rows[:, :, slots(c)], y[c][:])
+            nc.scalar.copy(y_bf[c][:], y[c][:].rearrange("p t j -> p j t"))
+
+        def hand_on(c):
+            quantize(y_codes, y_scales, y_bf[c][:], slots(c), E4M3)
+            nc.sync.dma_start(out_words[:, slots(c)], y_codes[:, slots(c)])
+
+        take_lagged(0)
+        take_lagged(1)
+        finish(0)
+        finish(1)
+        hand_on(0)
+        hand_on(1)
+        for q in range(4):
+            queue = nc.sync if q % 2 else nc.scalar
+            queue.dma_start(out_2[0, 4 * q : 4 * q + 4, :].bitcast(I32), y_scales[:].bitcast(I32)[32 * q : 32 * q + 4, :])

@@ -34,16 +34,17 @@ def tile_list_largerpicks_lagged_lagged_pl_kernel(tc, xf, fk, w_words, w_scales,
 
         list_a = pool.tile([P, J // 16], U16, name="list_a")
         list_b = pool.tile([P, J // 16], U16, name="list_b")
-        x = [pool.tile([P, T], F32, name="x%d" % t) for t in range(PACK)]
+        x = [pool.tile([P, T], F32, name="x%d" % t) for t in range(PACK - 1)]
         factor = pool.tile([P, PACK], F32, name="factor")
         w_raw = pool.tile([P, R], I32, name="w_raw")
         w_scale_raw = pool.tile([P, R], U8, name="w_scale_raw")
-        wb_raw = [pool.tile([P, PACK, N // 2], F32, name="wb_raw%d" % h) for h in range(2)]
-        resid = pool.tile([P, PACK, J], F32, name="resid")
         half_relu = pool.tile([P, J, PACK], F32, name="half_relu")
 
+        zeros = pool.tile([P, HID_LAG, PACK], F32, name="zeros", tag="reused3")
         nc.vector.memset(w_scale_raw[:].bitcast(I32), 0)
-        nc.vector.memset(half_relu[:, 0:HID_LAG, :], 0.0)
+        nc.vector.memset(zeros[:], 0.0)
+        nc.scalar.activation(half_relu[:, 0:HID_LAG, :], zeros[:], ACT.Relu, scale=0.5)
+        x.append(pool.tile([P, T], F32, name="x3", tag="reused3"))
 
         x_rows = xf.rearrange("(p t) n -> p t n", t=PACK)
         wb_rows = wb.rearrange("(p t) n -> p t n", t=PACK)
@@ -53,17 +54,14 @@ def tile_list_largerpicks_lagged_lagged_pl_kernel(tc, xf, fk, w_words, w_scales,
         nc.sync.dma_start(factor[:], fk.rearrange("(p t) o -> p (t o)", t=PACK))
         nc.sync.dma_start(x[1][:], x_rows[:, 1, :])
         nc.sync.dma_start(x[2][:], x_rows[:, 2, :])
+        nc.sync.dma_start(w_raw[:], w_words[0].rearrange("p n t -> p (n t)").bitcast(I32))
         for q in range(4):
             nc.sync.dma_start(w_scale_raw[:].bitcast(I32)[32 * q : 32 * q + 4, :], w_scales[0, 4 * q : 4 * q + 4, :].bitcast(I32))
         nc.sync.dma_start(x[3][:], x_rows[:, 3, :])
-        nc.sync.dma_start(w_raw[:], w_words[0].rearrange("p n t -> p (n t)").bitcast(I32))
-        for h in range(2):
-            nc.sync.dma_start(wb_raw[h][:], wb_rows[:, :, h * (N // 2) : (h + 1) * (N // 2)])
-        nc.sync.dma_start(resid[:], rs.rearrange("(p t) j -> p t j", t=PACK))
 
-        pick_a = [pool.tile([P, J], F32, name="pick_a%d" % t) for t in range(PACK)]
-        pick_b = [pool.tile([P, J], F32, name="pick_b%d" % t) for t in range(PACK)]
-        larger = [pool.tile([P, J], F32, name="larger%d" % t) for t in range(PACK)]
+        pick_a = [pool.tile([P, J], F32, name="pick_a%d" % t, tag="pick_a%d" % t if t else "reused0") for t in range(PACK)]
+        pick_b = [pool.tile([P, J], F32, name="pick_b%d" % t, tag="pick_b%d" % t if t else "reused1") for t in range(PACK)]
+        larger = [pool.tile([P, J], F32, name="larger%d" % t, tag="larger%d" % t if t else "reused2") for t in range(PACK)]
         u_bf = pool.tile([P, J, PACK], BF16, name="u_bf", align_bytes=64)
         u_codes = pool.tile([P, J], I32, name="u_codes", align_bytes=64)
         u_scales = pool.tile([P, J], U8, name="u_scales", align_bytes=64)
@@ -85,28 +83,35 @@ def tile_list_largerpicks_lagged_lagged_pl_kernel(tc, xf, fk, w_words, w_scales,
         every = slice(0, J)
         for t in range(PACK - 1):
             nc.scalar.activation(pick_a[t][:], x[t][:].indirect(list_a[:]), ACT.Copy)
-            nc.scalar.activation(pick_b[t][:, slots(1)], x[t][:].indirect(entries(list_b, 1)), ACT.Copy)
-            nc.vector.tensor_copy(pick_b[t][:, slots(0)], x[t][:].indirect(entries(list_b, 0)))
-            if t > 0:
+            if t == 0:
+                nc.vector.tensor_copy(pick_b[t][:], x[t][:].indirect(list_b[:]))
+            else:
+                nc.scalar.activation(pick_b[t][:, slots(1)], x[t][:].indirect(entries(list_b, 1)), ACT.Copy)
+                nc.vector.tensor_copy(pick_b[t][:, slots(0)], x[t][:].indirect(entries(list_b, 0)))
                 scale_and_round(t - 1, every)
             keep_larger(t, every)
+        wb_raw = [pool.tile([P, PACK, N // 2], F32, name="wb_raw%d" % h, tag="reused%d" % h) for h in range(2)]
+        resid = pool.tile([P, PACK, J], F32, name="resid", tag="reused2")
+        for h in range(2):
+            nc.sync.dma_start(wb_raw[h][:], wb_rows[:, :, h * (N // 2) : (h + 1) * (N // 2)])
+        nc.sync.dma_start(resid[:], rs.rearrange("(p t) j -> p t j", t=PACK))
         nc.vector.tensor_copy(
             w_scale[:].rearrange("p (t m) -> p t m", t=PACK), w_scale_raw[:].rearrange("p (m t) -> p t m", t=PACK)
         )
         last = PACK - 1
+        nc.vector.tensor_copy(
+            w_codes[:].rearrange("p (t c i) -> p c t i", t=PACK, i=4), w_raw[:].rearrange("p (c i t) -> p c t i", t=PACK, i=4)
+        )
         scale_and_round(last - 1, every)
         nc.scalar.activation(pick_a[last][:, slots(0)], x[last][:].indirect(entries(list_a, 0)), ACT.Copy)
-        nc.vector.tensor_copy(pick_b[last][:, slots(0)], x[last][:].indirect(entries(list_b, 0)))
+        nc.scalar.activation(pick_b[last][:, slots(0)], x[last][:].indirect(entries(list_b, 0)), ACT.Copy)
         nc.scalar.activation(pick_a[last][:, slots(1)], x[last][:].indirect(entries(list_a, 1)), ACT.Copy)
         nc.scalar.activation(pick_b[last][:, slots(1)], x[last][:].indirect(entries(list_b, 1)), ACT.Copy)
 
         keep_larger(last, slots(0))
         scale_and_round(last, slots(0))
-        nc.vector.tensor_copy(
-            w_codes[:].rearrange("p (t c i) -> p c t i", t=PACK, i=4), w_raw[:].rearrange("p (c i t) -> p c t i", t=PACK, i=4)
-        )
-        quantize(u_codes, u_scales, u_bf[:, slots(0), :], slots(0), E4M3)
         keep_larger(last, slots(1))
+        quantize(u_codes, u_scales, u_bf[:, slots(0), :], slots(0), E4M3)
         scale_and_round(last, slots(1))
         quantize(u_codes, u_scales, u_bf[:, slots(1), :], slots(1), E4M3)
 
@@ -132,8 +137,8 @@ def tile_list_largerpicks_lagged_lagged_pl_kernel(tc, xf, fk, w_words, w_scales,
         wb_codes = pool.tile([P, N], I32, name="wb_codes", align_bytes=64)
         wb_scales = pool.tile([P, N], U8, name="wb_scales", align_bytes=64)
 
-        def round_wb(h):
-            nc.scalar.copy(
+        def round_wb(h, copy):
+            copy(
                 wb_bf[:, :, h * 64 : (h + 1) * 64, :].rearrange("p t m i -> p m t i"),
                 wb_raw[h][:].rearrange("p i (m t) -> p m t i", t=PACK),
             )
@@ -152,15 +157,15 @@ def tile_list_largerpicks_lagged_lagged_pl_kernel(tc, xf, fk, w_words, w_scales,
 
         for c in range(CHUNKS):
             product(a_bank[c], w_codes, w_scale, E5M2, u_codes, u_scales, E4M3, c)
+        round_wb(0, nc.scalar.copy)
         relu_half(0)
-        round_wb(0)
         relu_half(1)
-        round_wb(1)
+        round_wb(1, nc.vector.tensor_copy)
         make_hid(0)
-        make_hid(1)
-        quantize(hid_codes, hid_scales, hid_bf[0][:], slots(0), E5M2)
-        quantize(hid_codes, hid_scales, hid_bf[1][:], slots(1), E5M2)
         nc.vector.quantize_mx(wb_codes[:].bitcast(E4M3), wb_scales[:], wb_bf[:].rearrange("p t m i -> p (t m i)"))
+        quantize(hid_codes, hid_scales, hid_bf[0][:], slots(0), E5M2)
+        make_hid(1)
+        quantize(hid_codes, hid_scales, hid_bf[1][:], slots(1), E5M2)
         for c in range(CHUNKS):
             product(p_bank[c], wb_codes, wb_scales, E4M3, hid_codes, hid_scales, E5M2, c)
 
@@ -171,24 +176,35 @@ def tile_list_largerpicks_lagged_lagged_pl_kernel(tc, xf, fk, w_words, w_scales,
         out_rows = out_0.rearrange("(p t) j -> p t j", t=PACK)
         out_words = out_1[0].rearrange("p c t -> p (c t)").bitcast(I32)
 
-        def take_lagged(c):
-            width = min(CHUNK, J - 1 - c * CHUNK)
-            cols = slice(c * CHUNK + 1, c * CHUNK + 1 + width)
-            nc.vector.scalar_tensor_tensor(resid[:, :, cols], p_bank[c][:, :, 0:width], -1.4, resid[:, :, cols], ALU.mult, ALU.add)
+        def take_lagged(c, first, width):
+            width = min(width, J - 1 - c * CHUNK - first)
+            cols = slice(c * CHUNK + first + 1, c * CHUNK + first + 1 + width)
+            nc.vector.scalar_tensor_tensor(
+                resid[:, :, cols], p_bank[c][:, :, first : first + width], -1.4, resid[:, :, cols], ALU.mult, ALU.add
+            )
 
-        def finish(c):
-            nc.vector.scalar_tensor_tensor(y[c][:], resid[:, :, slots(c)], 0.5, p_bank[c][:], ALU.mult, ALU.add)
+        def finish(c, first, width):
+            own = slice(first, first + width)
+            cols = slice(c * CHUNK + first, c * CHUNK + first + width)
+            nc.vector.scalar_tensor_tensor(y[c][:, :, own], resid[:, :, cols], 0.5, p_bank[c][:, :, own], ALU.mult, ALU.add)
+            nc.scalar.copy(y_bf[c][:, own, :], y[c][:, :, own].rearrange("p t j -> p j t"))
+
+        def store(c):
             nc.sync.dma_start(out_rows[:, :, slots(c)], y[c][:])
-            nc.scalar.copy(y_bf[c][:], y[c][:].rearrange("p t j -> p j t"))
 
         def hand_on(c):
             quantize(y_codes, y_scales, y_bf[c][:], slots(c), E4M3)
             nc.sync.dma_start(out_words[:, slots(c)], y_codes[:, slots(c)])
 
-        take_lagged(0)
-        take_lagged(1)
-        finish(0)
-        finish(1)
+        half = CHUNK // 2
+        take_lagged(0, 0, CHUNK)
+        finish(0, 0, CHUNK)
+        store(0)
+        take_lagged(1, 0, half)
+        take_lagged(1, half, half)
+        finish(1, 0, half)
+        finish(1, half, half)
+        store(1)
         hand_on(0)
         hand_on(1)
         for q in range(4):

@@ -21,6 +21,7 @@ CHUNK = 128
 CHUNKS = J // CHUNK
 LIST_COLS = CHUNK // 16
 HID_LAG = 2
+WB_SPLIT = 64
 
 
 def tile_list_largerpicks_lagged_lagged_pl_kernel(tc, xf, fk, w_words, w_scales, wb, rs, offs, offs2, out_0, out_1, out_2):
@@ -34,36 +35,33 @@ def tile_list_largerpicks_lagged_lagged_pl_kernel(tc, xf, fk, w_words, w_scales,
 
         list_a = pool.tile([P, J // 16], U16, name="list_a")
         list_b = pool.tile([P, J // 16], U16, name="list_b")
-        x = [pool.tile([P, T], F32, name="x%d" % t) for t in range(PACK - 1)]
+        x = [pool.tile([P, T], F32, name="x%d" % t) for t in range(PACK)]
         factor = pool.tile([P, PACK], F32, name="factor")
-        w_raw = pool.tile([P, R], I32, name="w_raw")
         w_scale_raw = pool.tile([P, R], U8, name="w_scale_raw")
-        half_relu = pool.tile([P, J, PACK], F32, name="half_relu")
 
-        zeros = pool.tile([P, HID_LAG, PACK], F32, name="zeros", tag="reused3")
-        nc.vector.memset(w_scale_raw[:].bitcast(I32), 0)
+        zeros = pool.tile([P, HID_LAG * PACK], F32, name="zeros")
+        pad = HID_LAG * PACK
+        shared = pool.tile([P, pad + PACK * PACK * WB_SPLIT], F32, name="shared", align_bytes=64)
         nc.vector.memset(zeros[:], 0.0)
-        nc.scalar.activation(half_relu[:, 0:HID_LAG, :], zeros[:], ACT.Relu, scale=0.5)
-        x.append(pool.tile([P, T], F32, name="x3", tag="reused3"))
+        nc.vector.memset(w_scale_raw[:].bitcast(I32), 0)
+        nc.scalar.dma_start(factor[:], fk.rearrange("(p t) o -> p (t o)", t=PACK))
+        nc.scalar.activation(shared[:, 0:pad], zeros[:], ACT.Relu, scale=0.5)
+        for q in range(4):
+            nc.scalar.dma_start(w_scale_raw[:].bitcast(I32)[32 * q : 32 * q + 4, :], w_scales[0, 4 * q : 4 * q + 4, :].bitcast(I32))
 
         x_rows = xf.rearrange("(p t) n -> p t n", t=PACK)
         wb_rows = wb.rearrange("(p t) n -> p t n", t=PACK)
-        nc.sync.dma_start(x[0][:], x_rows[:, 0, :])
         nc.sync.dma_start(list_a[:], offs)
         nc.sync.dma_start(list_b[:], offs2)
-        nc.sync.dma_start(factor[:], fk.rearrange("(p t) o -> p (t o)", t=PACK))
-        nc.sync.dma_start(x[1][:], x_rows[:, 1, :])
-        nc.sync.dma_start(x[2][:], x_rows[:, 2, :])
-        nc.sync.dma_start(w_raw[:], w_words[0].rearrange("p n t -> p (n t)").bitcast(I32))
-        for q in range(4):
-            nc.sync.dma_start(w_scale_raw[:].bitcast(I32)[32 * q : 32 * q + 4, :], w_scales[0, 4 * q : 4 * q + 4, :].bitcast(I32))
-        nc.sync.dma_start(x[3][:], x_rows[:, 3, :])
+        for t in range(PACK):
+            nc.sync.dma_start(x[t][:], x_rows[:, t, :])
 
-        pick_a = [pool.tile([P, J], F32, name="pick_a%d" % t, tag="pick_a%d" % t if t else "reused0") for t in range(PACK)]
-        pick_b = [pool.tile([P, J], F32, name="pick_b%d" % t, tag="pick_b%d" % t if t else "reused1") for t in range(PACK)]
-        larger = [pool.tile([P, J], F32, name="larger%d" % t, tag="larger%d" % t if t else "reused2") for t in range(PACK)]
+        pick_a = [pool.tile([P, J], F32, name="pick_a%d" % t, tag="pick_a%d" % t, align_bytes=64) for t in range(PACK)]
+        pick_b = [shared[:, pad : pad + J]]
+        pick_b.extend(pool.tile([P, J], F32, name="pick_b%d" % t, tag="pick_b%d" % t, align_bytes=64)[:] for t in range(1, PACK))
+        larger = pool.tile([P, PACK, J], F32, name="larger")
         u_bf = pool.tile([P, J, PACK], BF16, name="u_bf", align_bytes=64)
-        u_codes = pool.tile([P, J], I32, name="u_codes", align_bytes=64)
+        u_codes = [pool.tile([P, CHUNK], I32, name="u_codes0", align_bytes=64)]
         u_scales = pool.tile([P, J], U8, name="u_scales", align_bytes=64)
         w_codes = pool.tile([P, R], I32, name="w_codes", align_bytes=64)
         w_scale = pool.tile([P, R], U8, name="w_scale", align_bytes=64)
@@ -72,48 +70,64 @@ def tile_list_largerpicks_lagged_lagged_pl_kernel(tc, xf, fk, w_words, w_scales,
             return lst[:, c * LIST_COLS : (c + 1) * LIST_COLS]
 
         def keep_larger(t, cols):
-            nc.vector.tensor_tensor(larger[t][:, cols], pick_a[t][:, cols], pick_b[t][:, cols], ALU.max)
+            nc.vector.tensor_tensor(larger[:, t, cols], pick_a[t][:, cols], pick_b[t][:, cols], ALU.max)
 
-        def scale_and_round(t, cols):
-            nc.vector.tensor_scalar(u_bf[:, cols, t], larger[t][:, cols], factor[:, t : t + 1], None, ALU.mult)
+        def scale_and_round(c):
+            nc.vector.tensor_tensor(
+                u_bf[:, slots(c), :].rearrange("p (g i) t -> p g t i", i=4),
+                larger[:, :, slots(c)].rearrange("p t (g i) -> p g t i", i=4),
+                factor[:].rearrange("p (g t i) -> p g t i", g=1, i=1).to_broadcast([P, CHUNK // 4, PACK, 4]),
+                ALU.mult,
+            )
 
-        def quantize(codes, scales, src, cols, fmt):
-            nc.vector.quantize_mx(codes[:, cols].bitcast(fmt), scales[:, cols], src.rearrange("p j t -> p (j t)"))
+        def quantize(codes, scales, src, fmt):
+            nc.vector.quantize_mx(codes.bitcast(fmt), scales, src.rearrange("p j t -> p (j t)"))
 
         every = slice(0, J)
-        for t in range(PACK - 1):
-            nc.scalar.activation(pick_a[t][:], x[t][:].indirect(list_a[:]), ACT.Copy)
-            if t == 0:
-                nc.vector.tensor_copy(pick_b[t][:], x[t][:].indirect(list_b[:]))
-            else:
-                nc.scalar.activation(pick_b[t][:, slots(1)], x[t][:].indirect(entries(list_b, 1)), ACT.Copy)
-                nc.vector.tensor_copy(pick_b[t][:, slots(0)], x[t][:].indirect(entries(list_b, 0)))
-                scale_and_round(t - 1, every)
-            keep_larger(t, every)
-        wb_raw = [pool.tile([P, PACK, N // 2], F32, name="wb_raw%d" % h, tag="reused%d" % h) for h in range(2)]
-        resid = pool.tile([P, PACK, J], F32, name="resid", tag="reused2")
-        for h in range(2):
-            nc.sync.dma_start(wb_raw[h][:], wb_rows[:, :, h * (N // 2) : (h + 1) * (N // 2)])
-        nc.sync.dma_start(resid[:], rs.rearrange("(p t) j -> p t j", t=PACK))
-        nc.vector.tensor_copy(
-            w_scale[:].rearrange("p (t m) -> p t m", t=PACK), w_scale_raw[:].rearrange("p (m t) -> p t m", t=PACK)
-        )
         last = PACK - 1
+
+        def gather(on_vector, dst, t, offsets):
+            if on_vector:
+                nc.vector.tensor_copy(dst, x[t][:].indirect(offsets))
+            else:
+                nc.scalar.activation(dst, x[t][:].indirect(offsets), ACT.Copy)
+
+        for t in (0, 1):
+            gather(False, pick_a[t][:], t, list_a[:])
+            gather(True, pick_b[t], t, list_b[:])
+            if t == 1:
+                nc.vector.tensor_copy(
+                    w_scale[:].rearrange("p (t m) -> p t m", t=PACK), w_scale_raw[:].rearrange("p (m t) -> p t m", t=PACK)
+                )
+            keep_larger(t, every)
+        gather(False, pick_a[2][:], 2, list_a[:])
+        gather(False, pick_b[2][:, slots(1)], 2, entries(list_b, 1))
+        gather(True, pick_b[2][:, slots(0)], 2, entries(list_b, 0))
+        keep_larger(2, every)
+        for c in range(CHUNKS):
+            gather(False, pick_a[last][:, slots(c)], last, entries(list_a, c))
+            gather(False, pick_b[last][:, slots(c)], last, entries(list_b, c))
+
+        w_raw = pool.tile([P, R], I32, name="w_raw", tag="pick_a0", align_bytes=64)
+        wb_parts = [slice(0, WB_SPLIT), slice(WB_SPLIT, P)]
+        wb_raw = [
+            shared[:, pad:].rearrange("p (i n) -> p i n", i=PACK),
+            pool.tile([P, PACK, PACK * (P - WB_SPLIT)], F32, name="wb_raw1", tag="pick_a1", align_bytes=64)[:],
+        ]
+        resid = pool.tile([P, PACK, J], F32, name="resid", tag="pick_b1", align_bytes=64)
+        nc.sync.dma_start(w_raw[:], w_words[0].rearrange("p n t -> p (n t)").bitcast(I32))
+        for h, part in enumerate(wb_parts):
+            nc.sync.dma_start(wb_raw[h], wb_rows[:, :, PACK * part.start : PACK * part.stop])
+        nc.sync.dma_start(resid[:], rs.rearrange("(p t) j -> p t j", t=PACK))
+
+        keep_larger(last, slots(0))
         nc.vector.tensor_copy(
             w_codes[:].rearrange("p (t c i) -> p c t i", t=PACK, i=4), w_raw[:].rearrange("p (c i t) -> p c t i", t=PACK, i=4)
         )
-        scale_and_round(last - 1, every)
-        nc.scalar.activation(pick_a[last][:, slots(0)], x[last][:].indirect(entries(list_a, 0)), ACT.Copy)
-        nc.scalar.activation(pick_b[last][:, slots(0)], x[last][:].indirect(entries(list_b, 0)), ACT.Copy)
-        nc.scalar.activation(pick_a[last][:, slots(1)], x[last][:].indirect(entries(list_a, 1)), ACT.Copy)
-        nc.scalar.activation(pick_b[last][:, slots(1)], x[last][:].indirect(entries(list_b, 1)), ACT.Copy)
-
-        keep_larger(last, slots(0))
-        scale_and_round(last, slots(0))
+        scale_and_round(0)
         keep_larger(last, slots(1))
-        quantize(u_codes, u_scales, u_bf[:, slots(0), :], slots(0), E4M3)
-        scale_and_round(last, slots(1))
-        quantize(u_codes, u_scales, u_bf[:, slots(1), :], slots(1), E4M3)
+        quantize(u_codes[0][:], u_scales[:, slots(0)], u_bf[:, slots(0), :], E4M3)
+        scale_and_round(1)
 
         def product(bank, codes, scales, fmt, rhs_codes, rhs_scales, rhs_fmt, c):
             for t in range(PACK):
@@ -122,7 +136,7 @@ def tile_list_largerpicks_lagged_lagged_pl_kernel(tc, xf, fk, w_words, w_scales,
                     bank[:, t, :],
                     lhsT=codes[:, cols].bitcast(fmt),
                     lhsT_scale=scales[:, cols],
-                    rhs=rhs_codes[:, slots(c)].bitcast(rhs_fmt),
+                    rhs=rhs_codes.bitcast(rhs_fmt),
                     rhs_scale=rhs_scales[:, slots(c)],
                     start=True,
                     stop=True,
@@ -130,44 +144,51 @@ def tile_list_largerpicks_lagged_lagged_pl_kernel(tc, xf, fk, w_words, w_scales,
 
         a_bank = [psum.tile([P, PACK, CHUNK], F32, name="a_bank%d" % c) for c in range(CHUNKS)]
         p_bank = [psum.tile([P, PACK, CHUNK], F32, name="p_bank%d" % c) for c in range(CHUNKS)]
-        hid_bf = [pool.tile([P, CHUNK, PACK], BF16, name="hid_bf%d" % c, align_bytes=64) for c in range(CHUNKS)]
         hid_codes = pool.tile([P, J], I32, name="hid_codes", align_bytes=64)
         hid_scales = pool.tile([P, J], U8, name="hid_scales", align_bytes=64)
         wb_bf = pool.tile([P, PACK, P, PACK], BF16, name="wb_bf", align_bytes=64)
-        wb_codes = pool.tile([P, N], I32, name="wb_codes", align_bytes=64)
         wb_scales = pool.tile([P, N], U8, name="wb_scales", align_bytes=64)
 
-        def round_wb(h, copy):
+        def round_wb(copy, h):
             copy(
-                wb_bf[:, :, h * 64 : (h + 1) * 64, :].rearrange("p t m i -> p m t i"),
-                wb_raw[h][:].rearrange("p i (m t) -> p m t i", t=PACK),
+                wb_bf[:, :, wb_parts[h], :].rearrange("p t m i -> p m t i"),
+                wb_raw[h].rearrange("p i (m t) -> p m t i", t=PACK),
             )
 
-        def relu_half(c):
-            width = min(CHUNK, J - HID_LAG - c * CHUNK)
-            first = c * CHUNK + HID_LAG
-            nc.scalar.activation(
-                half_relu[:, first : first + width, :], a_bank[c][:, :, 0:width].rearrange("p t j -> p j t"), ACT.Relu, scale=0.5
-            )
+        wb_codes = pool.tile([P, N], I32, name="wb_codes", align_bytes=64)
 
-        def make_hid(c):
-            nc.vector.scalar_tensor_tensor(
-                hid_bf[c][:], a_bank[c][:].rearrange("p t j -> p j t"), 0.0, half_relu[:, slots(c), :], ALU.max, ALU.subtract
-            )
+        def quantize_wb(h):
+            cols = slice(h * N // 2, (h + 1) * N // 2)
+            quantize(wb_codes[:, cols], wb_scales[:, cols], wb_bf[:, 2 * h : 2 * h + 2, :, :].rearrange("p t m i -> p (t m) i"), E4M3)
 
+        def relu(dst, c, cols, scale):
+            nc.scalar.activation(dst, a_bank[c][:, :, cols].rearrange("p t j -> p j t"), ACT.Relu, scale=scale)
+
+        def make_hid(dst, c, cols, lagged):
+            nc.vector.scalar_tensor_tensor(dst, a_bank[c][:, :, cols].rearrange("p t j -> p j t"), 0.0, lagged, ALU.max, ALU.subtract)
+
+        round_wb(nc.scalar.copy, 0)
+        round_wb(nc.vector.tensor_copy, 1)
+        u_codes.append(pool.tile([P, CHUNK], I32, name="u_codes1", tag="pick_a1", align_bytes=64))
+        quantize(u_codes[1][:], u_scales[:, slots(1)], u_bf[:, slots(1), :], E4M3)
         for c in range(CHUNKS):
-            product(a_bank[c], w_codes, w_scale, E5M2, u_codes, u_scales, E4M3, c)
-        round_wb(0, nc.scalar.copy)
-        relu_half(0)
-        relu_half(1)
-        round_wb(1, nc.vector.tensor_copy)
-        make_hid(0)
-        nc.vector.quantize_mx(wb_codes[:].bitcast(E4M3), wb_scales[:], wb_bf[:].rearrange("p t m i -> p (t m i)"))
-        quantize(hid_codes, hid_scales, hid_bf[0][:], slots(0), E5M2)
-        make_hid(1)
-        quantize(hid_codes, hid_scales, hid_bf[1][:], slots(1), E5M2)
+            product(a_bank[c], w_codes, w_scale, E5M2, u_codes[c][:], u_scales, E4M3, c)
+        kept = CHUNK - HID_LAG
+        lag0 = shared[:, 0 : CHUNK * PACK].rearrange("p (j t) -> p j t", t=PACK)
+        lag1 = pool.tile([P, CHUNK, PACK], F32, name="lag1")
+        hid_bf = pool.tile([P, CHUNK, PACK], BF16, name="hid_bf", align_bytes=64)
+        relu(lag0[:, HID_LAG:, :], 0, slice(0, kept), 0.5)
+        quantize_wb(0)
+        make_hid(hid_bf[:], 0, slice(0, CHUNK), lag0)
+        relu(lag1[:, 0:HID_LAG, :], 0, slice(kept, CHUNK), 0.5)
+        relu(lag1[:, HID_LAG:, :], 1, slice(0, kept), 0.5)
+        quantize_wb(1)
+        quantize(hid_codes[:, slots(0)], hid_scales[:, slots(0)], hid_bf[:], E5M2)
+        hid_bf = pool.tile([P, CHUNK, PACK], BF16, name="hid_bf", align_bytes=64)
+        make_hid(hid_bf[:], 1, slice(0, CHUNK), lag1[:])
+        quantize(hid_codes[:, slots(1)], hid_scales[:, slots(1)], hid_bf[:], E5M2)
         for c in range(CHUNKS):
-            product(p_bank[c], wb_codes, wb_scales, E4M3, hid_codes, hid_scales, E5M2, c)
+            product(p_bank[c], wb_codes, wb_scales, E4M3, hid_codes[:, slots(c)], hid_scales, E5M2, c)
 
         y = [pool.tile([P, PACK, CHUNK], F32, name="y%d" % c) for c in range(CHUNKS)]
         y_bf = [pool.tile([P, CHUNK, PACK], BF16, name="y_bf%d" % c, align_bytes=64) for c in range(CHUNKS)]
@@ -187,13 +208,15 @@ def tile_list_largerpicks_lagged_lagged_pl_kernel(tc, xf, fk, w_words, w_scales,
             own = slice(first, first + width)
             cols = slice(c * CHUNK + first, c * CHUNK + first + width)
             nc.vector.scalar_tensor_tensor(y[c][:, :, own], resid[:, :, cols], 0.5, p_bank[c][:, :, own], ALU.mult, ALU.add)
-            nc.scalar.copy(y_bf[c][:, own, :], y[c][:, :, own].rearrange("p t j -> p j t"))
+            nc.scalar.copy(
+                y_bf[c][:, own, :].rearrange("p (g i) t -> p g t i", i=4), y[c][:, :, own].rearrange("p t (g i) -> p g t i", i=4)
+            )
 
         def store(c):
             nc.sync.dma_start(out_rows[:, :, slots(c)], y[c][:])
 
         def hand_on(c):
-            quantize(y_codes, y_scales, y_bf[c][:], slots(c), E4M3)
+            quantize(y_codes[:, slots(c)], y_scales[:, slots(c)], y_bf[c][:], E4M3)
             nc.sync.dma_start(out_words[:, slots(c)], y_codes[:, slots(c)])
 
         half = CHUNK // 2

from contextlib import ExitStack

import concourse.mybir as mybir

K, T, J, R, N = 512, 1024, 256, 512, 512
FLOPS = 2 * K * R * J + 2 * R * N * J

F32 = mybir.dt.float32
BF16 = mybir.dt.bfloat16
I32 = mybir.dt.int32
U16 = mybir.dt.uint16
U8 = mybir.dt.uint8
E4M3 = mybir.dt.float8_e4m3fn_x4
E5M2 = mybir.dt.float8_e5m2_x4
ALU = mybir.AluOpType
ACT = mybir.ActivationFunctionType

P = 128
PACK = 4
CHUNK = 128
CHUNKS = J // CHUNK
LIST_COLS = CHUNK // 16
HID_LAG = 2
WB_SPLIT = 64


def tile_list_largerpicks_lagged_lagged_pl_kernel(tc, xf, fk, w_words, w_scales, wb, rs, offs, offs2, out_0, out_1, out_2):
    nc = tc.nc
    with ExitStack() as ctx:
        pool = ctx.enter_context(tc.tile_pool(name="sbuf", bufs=1))
        psum = ctx.enter_context(tc.psum_pool(name="psum", bufs=1))

        def slots(c):
            return slice(c * CHUNK, (c + 1) * CHUNK)

        list_a = pool.tile([P, J // 16], U16, name="list_a")
        list_b = pool.tile([P, J // 16], U16, name="list_b")
        x = [pool.tile([P, T], F32, name="x%d" % t) for t in range(PACK)]
        factor = pool.tile([P, PACK], F32, name="factor")
        w_scale_raw = pool.tile([P, R], U8, name="w_scale_raw")

        zeros = pool.tile([P, HID_LAG * PACK], F32, name="zeros")
        pad = HID_LAG * PACK
        shared = pool.tile([P, pad + PACK * PACK * WB_SPLIT], F32, name="shared", align_bytes=64)
        nc.vector.memset(zeros[:], 0.0)
        nc.vector.memset(w_scale_raw[:].bitcast(I32), 0)
        nc.scalar.dma_start(factor[:], fk.rearrange("(p t) o -> p (t o)", t=PACK))
        nc.scalar.activation(shared[:, 0:pad], zeros[:], ACT.Relu, scale=0.5)
        for q in range(4):
            nc.scalar.dma_start(w_scale_raw[:].bitcast(I32)[32 * q : 32 * q + 4, :], w_scales[0, 4 * q : 4 * q + 4, :].bitcast(I32))

        x_rows = xf.rearrange("(p t) n -> p t n", t=PACK)
        wb_rows = wb.rearrange("(p t) n -> p t n", t=PACK)
        nc.sync.dma_start(list_a[:], offs)
        nc.sync.dma_start(list_b[:], offs2)
        for t in range(PACK):
            nc.sync.dma_start(x[t][:], x_rows[:, t, :])

        pick_a = [pool.tile([P, J], F32, name="pick_a%d" % t, tag="pick_a%d" % t, align_bytes=64) for t in range(PACK)]
        pick_b = [shared[:, pad : pad + J]]
        pick_b.extend(pool.tile([P, J], F32, name="pick_b%d" % t, tag="pick_b%d" % t, align_bytes=64)[:] for t in range(1, PACK))
        larger = pool.tile([P, PACK, J], F32, name="larger")
        u_bf = pool.tile([P, J, PACK], BF16, name="u_bf", align_bytes=64)
        u_codes = [pool.tile([P, CHUNK], I32, name="u_codes0", align_bytes=64)]
        u_scales = pool.tile([P, J], U8, name="u_scales", align_bytes=64)
        w_codes = pool.tile([P, R], I32, name="w_codes", align_bytes=64)
        w_scale = pool.tile([P, R], U8, name="w_scale", align_bytes=64)

        def entries(lst, c):
            return lst[:, c * LIST_COLS : (c + 1) * LIST_COLS]

        def keep_larger(t, cols):
            nc.vector.tensor_tensor(larger[:, t, cols], pick_a[t][:, cols], pick_b[t][:, cols], ALU.max)

        def scale_and_round(c):
            nc.vector.tensor_tensor(
                u_bf[:, slots(c), :].rearrange("p (g i) t -> p g t i", i=4),
                larger[:, :, slots(c)].rearrange("p t (g i) -> p g t i", i=4),
                factor[:].rearrange("p (g t i) -> p g t i", g=1, i=1).to_broadcast([P, CHUNK // 4, PACK, 4]),
                ALU.mult,
            )

        def quantize(codes, scales, src, fmt):
            nc.vector.quantize_mx(codes.bitcast(fmt), scales, src.rearrange("p j t -> p (j t)"))

        every = slice(0, J)
        last = PACK - 1

        def gather(on_vector, dst, t, offsets):
            if on_vector:
                nc.vector.tensor_copy(dst, x[t][:].indirect(offsets))
            else:
                nc.scalar.activation(dst, x[t][:].indirect(offsets), ACT.Copy)

        for t in (0, 1):
            gather(False, pick_a[t][:], t, list_a[:])
            gather(True, pick_b[t], t, list_b[:])
            if t == 1:
                nc.vector.tensor_copy(
                    w_scale[:].rearrange("p (t m) -> p t m", t=PACK), w_scale_raw[:].rearrange("p (m t) -> p t m", t=PACK)
                )
            keep_larger(t, every)
        gather(False, pick_a[2][:], 2, list_a[:])
        gather(False, pick_b[2][:, slots(1)], 2, entries(list_b, 1))
        gather(True, pick_b[2][:, slots(0)], 2, entries(list_b, 0))
        keep_larger(2, every)
        for c in range(CHUNKS):
            gather(False, pick_a[last][:, slots(c)], last, entries(list_a, c))
            gather(False, pick_b[last][:, slots(c)], last, entries(list_b, c))

        w_raw = pool.tile([P, R], I32, name="w_raw", tag="pick_a0", align_bytes=64)
        wb_parts = [slice(0, WB_SPLIT), slice(WB_SPLIT, P)]
        wb_raw = [
            shared[:, pad:].rearrange("p (i n) -> p i n", i=PACK),
            pool.tile([P, PACK, PACK * (P - WB_SPLIT)], F32, name="wb_raw1", tag="pick_a1", align_bytes=64)[:],
        ]
        resid = pool.tile([P, PACK, J], F32, name="resid", tag="pick_b1", align_bytes=64)
        nc.sync.dma_start(w_raw[:], w_words[0].rearrange("p n t -> p (n t)").bitcast(I32))
        for h, part in enumerate(wb_parts):
            nc.sync.dma_start(wb_raw[h], wb_rows[:, :, PACK * part.start : PACK * part.stop])
        nc.sync.dma_start(resid[:], rs.rearrange("(p t) j -> p t j", t=PACK))

        keep_larger(last, slots(0))
        nc.vector.tensor_copy(
            w_codes[:].rearrange("p (t c i) -> p c t i", t=PACK, i=4), w_raw[:].rearrange("p (c i t) -> p c t i", t=PACK, i=4)
        )
        scale_and_round(0)
        keep_larger(last, slots(1))
        quantize(u_codes[0][:], u_scales[:, slots(0)], u_bf[:, slots(0), :], E4M3)
        scale_and_round(1)

        def product(bank, codes, scales, fmt, rhs_codes, rhs_scales, rhs_fmt, c):
            for t in range(PACK):
                cols = slice(t * P, (t + 1) * P)
                nc.tensor.matmul_mx(
                    bank[:, t, :],
                    lhsT=codes[:, cols].bitcast(fmt),
                    lhsT_scale=scales[:, cols],
                    rhs=rhs_codes.bitcast(rhs_fmt),
                    rhs_scale=rhs_scales[:, slots(c)],
                    start=True,
                    stop=True,
                )

        a_bank = [psum.tile([P, PACK, CHUNK], F32, name="a_bank%d" % c) for c in range(CHUNKS)]
        p_bank = [psum.tile([P, PACK, CHUNK], F32, name="p_bank%d" % c) for c in range(CHUNKS)]
        hid_codes = pool.tile([P, J], I32, name="hid_codes", align_bytes=64)
        hid_scales = pool.tile([P, J], U8, name="hid_scales", align_bytes=64)
        wb_bf = pool.tile([P, PACK, P, PACK], BF16, name="wb_bf", align_bytes=64)
        wb_scales = pool.tile([P, N], U8, name="wb_scales", align_bytes=64)

        def round_wb(copy, h):
            copy(
                wb_bf[:, :, wb_parts[h], :].rearrange("p t m i -> p m t i"),
                wb_raw[h].rearrange("p i (m t) -> p m t i", t=PACK),
            )

        wb_codes = pool.tile([P, N], I32, name="wb_codes", align_bytes=64)

        def quantize_wb(h):
            cols = slice(h * N // 2, (h + 1) * N // 2)
            quantize(wb_codes[:, cols], wb_scales[:, cols], wb_bf[:, 2 * h : 2 * h + 2, :, :].rearrange("p t m i -> p (t m) i"), E4M3)

        def relu(dst, c, cols, scale):
            nc.scalar.activation(dst, a_bank[c][:, :, cols].rearrange("p t j -> p j t"), ACT.Relu, scale=scale)

        def make_hid(dst, c, cols, lagged):
            nc.vector.scalar_tensor_tensor(dst, a_bank[c][:, :, cols].rearrange("p t j -> p j t"), 0.0, lagged, ALU.max, ALU.subtract)

        round_wb(nc.scalar.copy, 0)
        round_wb(nc.vector.tensor_copy, 1)
        u_codes.append(pool.tile([P, CHUNK], I32, name="u_codes1", tag="pick_a1", align_bytes=64))
        quantize(u_codes[1][:], u_scales[:, slots(1)], u_bf[:, slots(1), :], E4M3)
        for c in range(CHUNKS):
            product(a_bank[c], w_codes, w_scale, E5M2, u_codes[c][:], u_scales, E4M3, c)
        kept = CHUNK - HID_LAG
        lag0 = shared[:, 0 : CHUNK * PACK].rearrange("p (j t) -> p j t", t=PACK)
        lag1 = pool.tile([P, CHUNK, PACK], F32, name="lag1")
        hid_bf = pool.tile([P, CHUNK, PACK], BF16, name="hid_bf", align_bytes=64)
        relu(lag0[:, HID_LAG:, :], 0, slice(0, kept), 0.5)
        quantize_wb(0)
        make_hid(hid_bf[:], 0, slice(0, CHUNK), lag0)
        relu(lag1[:, 0:HID_LAG, :], 0, slice(kept, CHUNK), 0.5)
        relu(lag1[:, HID_LAG:, :], 1, slice(0, kept), 0.5)
        quantize_wb(1)
        quantize(hid_codes[:, slots(0)], hid_scales[:, slots(0)], hid_bf[:], E5M2)
        hid_bf = pool.tile([P, CHUNK, PACK], BF16, name="hid_bf", align_bytes=64)
        make_hid(hid_bf[:], 1, slice(0, CHUNK), lag1[:])
        quantize(hid_codes[:, slots(1)], hid_scales[:, slots(1)], hid_bf[:], E5M2)
        for c in range(CHUNKS):
            product(p_bank[c], wb_codes, wb_scales, E4M3, hid_codes[:, slots(c)], hid_scales, E5M2, c)

        y = [pool.tile([P, PACK, CHUNK], F32, name="y%d" % c) for c in range(CHUNKS)]
        y_bf = [pool.tile([P, CHUNK, PACK], BF16, name="y_bf%d" % c, align_bytes=64) for c in range(CHUNKS)]
        y_codes = pool.tile([P, J], I32, name="y_codes", align_bytes=64)
        y_scales = pool.tile([P, J], U8, name="y_scales", align_bytes=64)
        out_rows = out_0.rearrange("(p t) j -> p t j", t=PACK)
        out_words = out_1[0].rearrange("p c t -> p (c t)").bitcast(I32)

        def take_lagged(c, first, width):
            width = min(width, J - 1 - c * CHUNK - first)
            cols = slice(c * CHUNK + first + 1, c * CHUNK + first + 1 + width)
            nc.vector.scalar_tensor_tensor(
                resid[:, :, cols], p_bank[c][:, :, first : first + width], -1.4, resid[:, :, cols], ALU.mult, ALU.add
            )

        def finish(c, first, width):
            own = slice(first, first + width)
            cols = slice(c * CHUNK + first, c * CHUNK + first + width)
            nc.vector.scalar_tensor_tensor(y[c][:, :, own], resid[:, :, cols], 0.5, p_bank[c][:, :, own], ALU.mult, ALU.add)
            nc.scalar.copy(
                y_bf[c][:, own, :].rearrange("p (g i) t -> p g t i", i=4), y[c][:, :, own].rearrange("p t (g i) -> p g t i", i=4)
            )

        def store(c):
            nc.sync.dma_start(out_rows[:, :, slots(c)], y[c][:])

        def hand_on(c):
            quantize(y_codes[:, slots(c)], y_scales[:, slots(c)], y_bf[c][:], E4M3)
            nc.sync.dma_start(out_words[:, slots(c)], y_codes[:, slots(c)])

        half = CHUNK // 2
        take_lagged(0, 0, CHUNK)
        finish(0, 0, CHUNK)
        store(0)
        take_lagged(1, 0, half)
        take_lagged(1, half, half)
        finish(1, 0, half)
        finish(1, half, half)
        store(1)
        hand_on(0)
        hand_on(1)
        for q in range(4):
            queue = nc.sync if q % 2 else nc.scalar
            queue.dma_start(out_2[0, 4 * q : 4 * q + 4, :].bitcast(I32), y_scales[:].bitcast(I32)[32 * q : 32 * q + 4, :])
